import numpy as np, ml_dtypes
CORES = [24,40,56,80,88,96]
N = 6
import mx_ref
NC, WB = 128, 2
D = 2 * WB + 1
BF = ml_dtypes.bfloat16
def setup_inputs(rng):
    def f(*shape):
        return mx_ref.flush((rng.standard_normal(shape, dtype=np.float32) * np.exp2(rng.integers(-2, 3, shape[:-1] + (1,)))).astype(BF))
    return {"w": f(N, 128, 512), "x": f(N, 128, 4 * NC)}
def setup_inputs_blocks(rng):
    d = setup_inputs(rng)
    for k in ("w", "x"): d[k] = mx_ref.spread(d[k], rng, 4)
    return d
def setup_inputs_wide(rng):
    d = setup_inputs(rng)
    for k in ("w", "x"): d[k] = mx_ref.flush((d[k].astype(np.float32) * np.exp2(rng.integers(-8, 9, (N, 1, 1))).astype(np.float32)).astype(BF))
    return d
def setup_inputs_zeros(rng):
    d = setup_inputs(rng); v = d["x"].reshape(N, 128, -1, 4).copy()
    v[np.broadcast_to((rng.random((N, 1, v.shape[2], 1)) < 0.33), v.shape)] = 0
    d["x"] = v.reshape(d["x"].shape)
    return d
def reference(w, x):
    QX = [mx_ref.quantize(x[j]) for j in range(N)]
    y = np.zeros((N, 128, D * NC), np.float32)
    for r in range(N):
        qw = mx_ref.quantize(w[r])
        for i in range(D):
            y[r][:, NC * i:NC * i + NC] = mx_ref.matmul(qw, QX[(r + i - WB) % N])
    return {"y": y}

from concourse.bass import DstId, RemoteDMATransfer
from concourse.mybir import dt, ActivationFunctionType

N = 6
NC = 128
WB = 2
D = 2 * WB + 1

SCRATCH = {
    "xb": ("sbuf", [128, 4 * NC], "bfloat16"),
    "wb": ("sbuf", [128, 4 * NC], "bfloat16"),
    "qw": ("sbuf", [128, NC], "float8_e4m3fn_x4"),
    "sw": ("sbuf", [128, NC], "uint8"),
    "qx": ("sbuf", [128, N * NC], "float8_e4m3fn_x4"),
    "sx": ("sbuf", [128, N * NC], "uint8"),
    "acc": ("psum", [128, 512 * D], "float32"),
    "ysb": ("sbuf", [128, D * NC], "float32"),
}
SEMAPHORES = (["lx", "lw", "zx", "zw", "rp", "rc", "ls", "st"]
              + ["a%d" % j for j in range(N)] + ["m%d" % i for i in range(D)] + ["c%d" % i for i in range(D)])

ALL_ENGINES_FROM = 3
_MEMO = {}


def _bits(m):
    return [b for b in range(m.bit_length()) if (m >> b) & 1]


def _take(m, k):
    return sum(1 << b for b in _bits(m)[:k])


def _pow2(m):
    k = 1
    while 2 * k <= len(_bits(m)):
        k *= 2
    return _take(m, k)


def _plan(T, topo):
    if "plan" in _MEMO:
        return _MEMO["plan"]
    cores = list(T.cores)
    n = len(cores)
    want = {j: [(j + k) % n for k in range(-WB, WB + 1) if k] for j in range(n)}
    direct = {j: [r for r in want[j] if topo.may_write(cores[j], cores[r])] for j in range(n)}
    cross = {j: [r for r in want[j] if r not in direct[j]] for j in range(n)}

    def perms(v):
        if len(v) <= 1:
            return [list(v)]
        return [[v[k]] + p for k in range(len(v)) for p in perms(v[:k] + v[k + 1:])]

    def search(j, chosen):
        if j == n:
            hits = 0
            for t in range(2 * WB):
                aims = [chosen[a][t] for a in range(n) if t < len(chosen[a])]
                hits += len(aims) - len(set(aims))
            return hits, [list(v) for v in chosen]
        return min((search(j + 1, chosen + [p]) for p in perms(direct[j])), key=lambda a: a[0])
    sched = dict(enumerate(search(0, [])[1]))

    chip_of = {j: topo.chip(cores[j]) for j in range(n)}
    mate_of = {j: [x for x in range(topo.CHIPS) if topo.mates(chip_of[j], x)][0] for j in range(n)}
    base = {}
    for j in range(n):
        for r in direct[j]:
            for k in (("out", chip_of[j], topo.die(cores[j])), ("in", chip_of[r], topo.die(cores[j]))):
                base[k] = base.get(k, 0) + 0.3
    every = range(topo.CHIPS * topo.CORES_PER_CHIP)
    flows = [(j, r) for j in range(n) for r in cross[j]]
    cand = {(j, r): [c for c in every if topo.chip(c) == chip_of[j] and T.rank_of(c) is None
                     and topo.may_write(c, cores[r])] for j, r in flows}

    def links(j, r, d):
        if topo.mates(chip_of[j], chip_of[r]):
            return [("mate", chip_of[j], d)]
        return [("mate", chip_of[j], d), ("out", mate_of[j], d), ("in", chip_of[r], d)]

    def place(k, load, used):
        if k == len(flows):
            return sum(v * v for v in load.values()), []
        j, r = flows[k]
        best = None
        for d in sorted(set(topo.die(c) for c in cand[(j, r)]), key=lambda q: q != topo.die(cores[j])):
            free = [c for c in cand[(j, r)] if topo.die(c) == d and c not in used]
            if not free:
                continue
            more = dict(load)
            for q in links(j, r, d):
                more[q] = more.get(q, 0) + 1
            cost, tail = place(k + 1, more, used | {free[0]})
            cost += 0.01 * (d != topo.die(cores[j]))
            if best is None or cost < best[0] - 1e-9:
                best = (cost, [free[0]] + tail)
        return best
    chosen = dict(zip(flows, place(0, base, frozenset())[1]))
    relay = {j: [(chosen[(j, r)], r) for r in sorted(cross[j], key=lambda q: topo.mates(chip_of[j], chip_of[q]))]
             for j in range(n)}

    order = {}
    for r in range(n):
        key = {r: (0, 0, 0)}
        for j in range(n):
            if r in sched[j]:
                key[j] = (1, sched[j].index(r) + (len(relay[j]) if len(relay[j]) >= ALL_ENGINES_FROM else 0), j)
            for pos, (c, rr) in enumerate(relay[j]):
                if rr == r:
                    key[j] = (2, pos, j)
        order[r] = sorted(key, key=lambda a: key[a])
    _MEMO["plan"] = (sched, relay, order)
    return _MEMO["plan"]


def _direct_mask(topo, cores, j, direct):
    m = None
    for q in direct[j]:
        mm = topo.mask(cores[j], cores[q])
        m = mm if m is None else (m & mm)
    return _pow2(m)


def _handover_mask(topo, cores, j, direct, relay):
    m = None
    for c, _ in relay[j]:
        mm = topo.mask(cores[j], c)
        m = mm if m is None else (m & mm)
    if len(relay[j]) >= ALL_ENGINES_FROM or not direct[j]:
        return _pow2(m)
    rest = m & ~_direct_mask(topo, cores, j, direct)
    return _pow2(rest if rest else m)


def _send(g, T, topo, dst_cores, j, mask, sem, which):
    lo, hi = j * NC, (j + 1) * NC
    ap = T.sx[:, lo:hi] if which == "plane" else T.qx[:, lo:hi].bitcast(dt.uint8)
    ids = []
    for c in dst_cores:
        rid, pid, _ = topo.addr(c)
        ids.append(DstId(rid=rid, pnc=pid))
    g.remote_dma_fused([RemoteDMATransfer(dst_ids=ids, dma_engine_mask=mask, remote_sem=sem,
                                          srcs=[ap], dsts=[ap for _ in dst_cores])], local_sem=T.sem.ls)
    return len(_bits(mask))


def rank_program(g, core, T, topo):
    direct, relay, order = _plan(T, topo)
    cores = list(T.cores)
    n = len(cores)
    rank = T.rank_of(core)

    if rank is None:
        for j in range(n):
            for c, r in relay[j]:
                if c != core:
                    continue
                got = len(_bits(_handover_mask(topo, cores, j, direct, relay)))
                m = _pow2(topo.mask(core, cores[r]))
                a = T.sem["a%d" % j]
                g.wait_ge(T.sem.rp, got)
                sent = _send(g, T, topo, [cores[r]], j, m, a, "plane")
                g.wait_ge(T.sem.rc, got)
                sent += _send(g, T, topo, [cores[r]], j, m, a, "codes")
                g.wait_ge(T.sem.ls, sent)
        return

    r = rank
    lo, hi = r * NC, (r + 1) * NC
    g.sync.dma_start(T.xb[:], T.x[:]).then_inc(T.sem.lx, 16)
    g.sync.dma_start(T.wb[:], T.w[:]).then_inc(T.sem.lw, 16)
    g.vector.wait_ge(T.sem.lx, 16)
    g.vector.quantize_mx(T.qx[:, lo:hi], T.sx[:, lo:hi], T.xb[:]).then_inc(T.sem.zx, 1)
    g.vector.wait_ge(T.sem.lw, 16)
    g.vector.quantize_mx(T.qw[:], T.sw[:], T.wb[:]).then_inc(T.sem.zw, 1)

    g.wait_ge(T.sem.zx, 1)
    sent = 0
    a = T.sem["a%d" % r]
    rel = [c for c, _ in relay[r]]
    if rel:
        m = _handover_mask(topo, cores, r, direct, relay)
        sent += _send(g, T, topo, rel, r, m, T.sem.rp, "plane")
        sent += _send(g, T, topo, rel, r, m, T.sem.rc, "codes")
    if direct[r]:
        dst = [cores[q] for q in direct[r]]
        m = _direct_mask(topo, cores, r, direct)
        sent += _send(g, T, topo, dst, r, m, a, "plane")
        sent += _send(g, T, topo, dst, r, m, a, "codes")
    g.wait_ge(T.sem.ls, sent)

    g.tensor.wait_ge(T.sem.zw, 1)
    for k, j in enumerate(order[r]):
        i = (j - r + WB) % n
        if j == r:
            g.tensor.wait_ge(T.sem.zx, 1)
        else:
            if r in direct[j]:
                per = len(_bits(_direct_mask(topo, cores, j, direct)))
            else:
                c = [c for c, q in relay[j] if q == r][0]
                per = len(_bits(_pow2(topo.mask(c, core))))
            g.tensor.wait_ge(T.sem["a%d" % j], 2 * per)
        ps, sb, yy = T.acc[:, 512 * i:512 * i + NC], T.ysb[:, i * NC:(i + 1) * NC], T.y[:, i * NC:(i + 1) * NC]
        g.tensor.matmul_mx(ps, T.qw[:], T.sw[:], T.qx[:, j * NC:(j + 1) * NC], T.sx[:, j * NC:(j + 1) * NC],
                           True, True).then_inc(T.sem["m%d" % i], 1)
        if (len(order[r]) - 1 - k) % 2 == 0:
            g.vector.wait_ge(T.sem["m%d" % i], 1)
            g.vector.tensor_copy(sb, ps).then_inc(T.sem["c%d" % i], 1)
            g.sync.wait_ge(T.sem["c%d" % i], 1)
            g.sync.dma_start(yy, sb).then_inc(T.sem.st, 16)
        else:
            g.scalar.wait_ge(T.sem["m%d" % i], 1)
            g.scalar.activation(sb, ps, ActivationFunctionType.Copy).then_inc(T.sem["c%d" % i], 1)
            g.scalar.wait_ge(T.sem["c%d" % i], 1)
            g.scalar.dma_start(yy, sb).then_inc(T.sem.st, 16)
    g.sync.wait_ge(T.sem.st, 16 * len(order[r]))
